import numpy as np, ml_dtypes
CORES = [29,2,10,18,34,42,50,58,66,74,82,90,98,106,114,122]
N = 16
ROOT = 0
def setup_inputs(rng):
    return {"x": rng.standard_normal((N, 128, 2048), dtype=np.float32).astype(ml_dtypes.bfloat16)}
def reference(x):
    return {"y": np.broadcast_to(x[ROOT], x.shape)}

@@ -1,0 +1,108 @@
+import concourse.bass as bass
+import comms_topo
+FAR = 4
+ROOT = 29
+RANKS = [8 * ch + 2 for ch in range(16) if ch != 3]
+EVEN_R = [r for r in RANKS if r // 8 % 2 == 0]
+ODD_R = [r for r in RANKS if r // 8 % 2 == 1]
+ODD = [1, 5, 7, 9, 11, 13, 15]
+HELP = [30, 26, 31, 27]
+SIDE = [24, 25, 24, 25]
+
+def eng(lo, n):
+    return (1 << n) - 1 << lo
+
+def finish(prog, groups):
+    for r in RANKS:
+        for j, (b, lo, hi) in enumerate(groups):
+            prog[r].append(('W', 'g%d' % j))
+            prog[r].append(('ST', b, lo, hi))
+        prog[r].append(('W', 'st'))
+    for c in prog:
+        if any((op[0] == 'S' for op in prog[c])):
+            prog[c].append(('W', 'sent'))
+    tot = {}
+    for c in prog:
+        for op in prog[c]:
+            if op[0] == 'S':
+                for p, dsts, mask, sem in op[1]:
+                    n = bin(mask).count('1')
+                    tot[c, 'sent'] = tot.get((c, 'sent'), 0) + n
+                    for d in dsts:
+                        tot[d, sem] = tot.get((d, sem), 0) + n
+            elif op[0] == 'LD':
+                tot[c, op[4]] = tot.get((c, op[4]), 0) + 16
+            elif op[0] in ('ST', 'XY'):
+                tot[c, 'st'] = tot.get((c, 'st'), 0) + 16
+    return (prog, tot)
+
+def resend(core, piece, gname, far):
+    if not far:
+        return [(piece, [r for r in RANKS if r > core] + [r for r in RANKS if r < core], 255, gname)]
+    ev = [r for r in EVEN_R if r > core] + [r for r in EVEN_R if r < core]
+    od = [r for r in ODD_R if r > core] + [r for r in ODD_R if r < core]
+    w = 8 // far
+    return [(piece, ev[s::far] + od[s::far], eng(s * w, w), gname) for s in range(far)]
+
+def build(far):
+    counts_o = [8, 8, 8, 4]
+    counts = [12, 8, 8, 4]
+    prog = {c: [] for c in range(128)}
+    root = prog[ROOT]
+    for q in range(4):
+        root.append(('LD', q, 0, counts[q], 'ld%d' % q))
+    groups = [(0, 0, 4), (0, 4, 12), (1, 0, 8), (2, 0, 8), (3, 0, 4)]
+    first = [((0, i), [HELP[i], SIDE[i]], eng(8 + 2 * i, 2), 'pc') for i in range(4)]
+    n = max(1, far)
+    m = max(1, far // 2)
+    for i in range(4):
+        prog[HELP[i]].append(('W', 'pc'))
+        prog[HELP[i]].append(('S', [((0, i), EVEN_R[s::n], eng(s * (8 // n), 8 // n), 'g0') for s in range(n)]))
+    for s in range(2):
+        prog[24 + s].append(('W', 'pc'))
+        prog[24 + s].append(('S', [((0, s + 2 * a), ODD_R[b::m], eng((a * m + b) * (4 // m), 4 // m), 'g0') for a in range(2) for b in range(m)]))
+    k = 0
+    for q in range(4):
+        base = 4 if q == 0 else 0
+        wo = 8 // counts_o[q]
+        trs = list(first) if q == 0 else []
+        for i in range(counts_o[q]):
+            core = 8 * ODD[k % 7] + [2, 6, 3, 7][k // 7]
+            k += 1
+            trs.append(((q, base + i), [core], eng(i * wo, wo), 'pc'))
+            prog[core].append(('W', 'pc'))
+            prog[core].append(('S', resend(core, (q, base + i), 'g%d' % (q + 1), far)))
+        root.append(('W', 'ld%d' % q))
+        root.append(('S', trs))
+    root.append(('XY',))
+    root.append(('W', 'st'))
+    return ([64, 64, 64, 64], counts) + finish(prog, groups)
+NCOLS, COUNTS, PROG, TOTAL = build(FAR)
+ROW0 = [0]
+for q in range(4):
+    ROW0.append(ROW0[q] + COUNTS[q] * NCOLS[q] // 16)
+SCRATCH = {'bufa': ('dram', [COUNTS[0], 128, NCOLS[0]], 'bfloat16'), 'bufb': ('dram', [COUNTS[1], 128, NCOLS[1]], 'bfloat16'), 'bufc': ('dram', [COUNTS[2], 128, NCOLS[2]], 'bfloat16'), 'bufd': ('dram', [COUNTS[3], 128, NCOLS[3]], 'bfloat16')}
+SEMAPHORES = ['ld0', 'ld1', 'ld2', 'ld3', 'st', 'sent', 'pc', 'g0', 'g1', 'g2', 'g3', 'g4']
+
+def rank_program(g, core, T, topo):
+    sems = {'ld0': T.sem.ld0, 'ld1': T.sem.ld1, 'ld2': T.sem.ld2, 'ld3': T.sem.ld3, 'st': T.sem.st, 'sent': T.sem.sent, 'pc': T.sem.pc, 'g0': T.sem.g0, 'g1': T.sem.g1, 'g2': T.sem.g2, 'g3': T.sem.g3, 'g4': T.sem.g4}
+    bufs = [T.bufa, T.bufb, T.bufc, T.bufd]
+    for op in PROG[core]:
+        if op[0] == 'W':
+            g.wait_ge(sems[op[1]], TOTAL[core, op[1]])
+        elif op[0] in ('LD', 'ST'):
+            b, lo, hi = (op[1], op[2], op[3])
+            r0 = ROW0[b] + lo * NCOLS[b] // 16
+            r1 = ROW0[b] + hi * NCOLS[b] // 16
+            if op[0] == 'LD':
+                g.dma_start(bufs[b][lo:hi], T.x[r0:r1, :]).then_inc(sems[op[4]], 16)
+            else:
+                g.dma_start(T.y[r0:r1, :], bufs[b][lo:hi]).then_inc(sems['st'], 16)
+        elif op[0] == 'XY':
+            g.dma_start(T.y[:, :], T.x[:, :]).then_inc(sems['st'], 16)
+        else:
+            trs = []
+            for (b, s), dsts, mask, sem in op[1]:
+                ids = [bass.DstId(rid=topo.addr(d)[0], pnc=topo.addr(d)[1]) for d in dsts]
+                trs.append(bass.RemoteDMATransfer(dst_ids=ids, dma_engine_mask=mask, remote_sem=sems[sem], srcs=[bufs[b][s]], dsts=[bufs[b][s] for d in dsts], alu_op=0))
+            g.remote_dma_fused(trs, local_sem=sems['sent'])

@@ -1,6 +1,6 @@
 import concourse.bass as bass
 import comms_topo
-FAR = 4
+
 ROOT = 29
 RANKS = [8 * ch + 2 for ch in range(16) if ch != 3]
 EVEN_R = [r for r in RANKS if r // 8 % 2 == 0]
@@ -8,101 +8,128 @@ ODD_R = [r for r in RANKS if r // 8 % 2 == 1]
 ODD = [1, 5, 7, 9, 11, 13, 15]
 HELP = [30, 26, 31, 27]
 SIDE = [24, 25, 24, 25]
+NP = 32
+NCOL = 64
+RPP = 128 // NP
+FAR = 4
+CHUNKS = [12, 8, 8, 4]
+G, SY, SC = 0, 1, 2
+
 
 def eng(lo, n):
     return (1 << n) - 1 << lo
 
-def finish(prog, groups):
-    for r in RANKS:
-        for j, (b, lo, hi) in enumerate(groups):
-            prog[r].append(('W', 'g%d' % j))
-            prog[r].append(('ST', b, lo, hi))
-        prog[r].append(('W', 'st'))
-    for c in prog:
-        if any((op[0] == 'S' for op in prog[c])):
-            prog[c].append(('W', 'sent'))
-    tot = {}
-    for c in prog:
-        for op in prog[c]:
-            if op[0] == 'S':
-                for p, dsts, mask, sem in op[1]:
-                    n = bin(mask).count('1')
-                    tot[c, 'sent'] = tot.get((c, 'sent'), 0) + n
-                    for d in dsts:
-                        tot[d, sem] = tot.get((d, sem), 0) + n
-            elif op[0] == 'LD':
-                tot[c, op[4]] = tot.get((c, op[4]), 0) + 16
-            elif op[0] in ('ST', 'XY'):
-                tot[c, 'st'] = tot.get((c, 'st'), 0) + 16
-    return (prog, tot)
 
-def resend(core, piece, gname, far):
-    if not far:
-        return [(piece, [r for r in RANKS if r > core] + [r for r in RANKS if r < core], 255, gname)]
-    ev = [r for r in EVEN_R if r > core] + [r for r in EVEN_R if r < core]
-    od = [r for r in ODD_R if r > core] + [r for r in ODD_R if r < core]
-    w = 8 // far
-    return [(piece, ev[s::far] + od[s::far], eng(s * w, w), gname) for s in range(far)]
+def rot(lst, core):
+    return [r for r in lst if r > core] + [r for r in lst if r < core]
 
-def build(far):
-    counts_o = [8, 8, 8, 4]
-    counts = [12, 8, 8, 4]
+
+def resend(core, piece, gname):
+    ev, od = rot(EVEN_R, core), rot(ODD_R, core)
+    w = 8 // FAR
+    return [(piece, ev[s::FAR] + od[s::FAR], eng(s * w, w), gname) for s in range(FAR)]
+
+
+def build():
     prog = {c: [] for c in range(128)}
     root = prog[ROOT]
-    for q in range(4):
-        root.append(('LD', q, 0, counts[q], 'ld%d' % q))
-    groups = [(0, 0, 4), (0, 4, 12), (1, 0, 8), (2, 0, 8), (3, 0, 4)]
-    first = [((0, i), [HELP[i], SIDE[i]], eng(8 + 2 * i, 2), 'pc') for i in range(4)]
-    n = max(1, far)
-    m = max(1, far // 2)
+    lo = 0
+    bounds = []
+    for q, n in enumerate(CHUNKS):
+        root.append((SY if q % 2 == 0 else SC, 'LD', lo, lo + n, 'ld%d' % q))
+        bounds.append((lo, lo + n))
+        lo += n
+    groups = [(0, 4), (4, 12), (12, 20), (20, 28), (28, 32)]
+    first = [(i, [HELP[i], SIDE[i]], eng(8 + 2 * i, 2), 'pc') for i in range(4)]
     for i in range(4):
-        prog[HELP[i]].append(('W', 'pc'))
-        prog[HELP[i]].append(('S', [((0, i), EVEN_R[s::n], eng(s * (8 // n), 8 // n), 'g0') for s in range(n)]))
+        prog[HELP[i]].append((G, 'W', 'pc'))
+        prog[HELP[i]].append((G, 'S', [(i, EVEN_R[s::4], eng(s * 2, 2), 'g0') for s in range(4)]))
     for s in range(2):
-        prog[24 + s].append(('W', 'pc'))
-        prog[24 + s].append(('S', [((0, s + 2 * a), ODD_R[b::m], eng((a * m + b) * (4 // m), 4 // m), 'g0') for a in range(2) for b in range(m)]))
+        prog[24 + s].append((G, 'W', 'pc'))
+        prog[24 + s].append((G, 'S', [(s + 2 * a, ODD_R[b::2], eng((a * 2 + b) * 2, 2), 'g0')
+                                      for a in range(2) for b in range(2)]))
     k = 0
-    for q in range(4):
-        base = 4 if q == 0 else 0
-        wo = 8 // counts_o[q]
+    for q, (a, b) in enumerate(bounds):
+        base = a + 4 if q == 0 else a
+        cnt = b - base
+        wo = 8 // cnt
         trs = list(first) if q == 0 else []
-        for i in range(counts_o[q]):
+        for i in range(cnt):
             core = 8 * ODD[k % 7] + [2, 6, 3, 7][k // 7]
             k += 1
-            trs.append(((q, base + i), [core], eng(i * wo, wo), 'pc'))
-            prog[core].append(('W', 'pc'))
-            prog[core].append(('S', resend(core, (q, base + i), 'g%d' % (q + 1), far)))
-        root.append(('W', 'ld%d' % q))
-        root.append(('S', trs))
-    root.append(('XY',))
-    root.append(('W', 'st'))
-    return ([64, 64, 64, 64], counts) + finish(prog, groups)
-NCOLS, COUNTS, PROG, TOTAL = build(FAR)
-ROW0 = [0]
-for q in range(4):
-    ROW0.append(ROW0[q] + COUNTS[q] * NCOLS[q] // 16)
-SCRATCH = {'bufa': ('dram', [COUNTS[0], 128, NCOLS[0]], 'bfloat16'), 'bufb': ('dram', [COUNTS[1], 128, NCOLS[1]], 'bfloat16'), 'bufc': ('dram', [COUNTS[2], 128, NCOLS[2]], 'bfloat16'), 'bufd': ('dram', [COUNTS[3], 128, NCOLS[3]], 'bfloat16')}
-SEMAPHORES = ['ld0', 'ld1', 'ld2', 'ld3', 'st', 'sent', 'pc', 'g0', 'g1', 'g2', 'g3', 'g4']
+            trs.append((base + i, [core], eng(i * wo, wo), 'pc'))
+            prog[core].append((G, 'W', 'pc'))
+            if core in RANKS:
+                prog[core].append((SY, 'W', 'pc'))
+                prog[core].append((SC, 'W', 'pc'))
+            prog[core].append((G, 'S', resend(core, base + i, 'g%d' % (q + 1))))
+        root.append((G, 'W', 'ld%d' % q))
+        root.append((G, 'S', trs))
+    root.append((G, 'INC', 'go'))
+    root.append((SY, 'W', 'go'))
+    root.append((SY, 'XY'))
+    root.append((G, 'W', 'st'))
+    for r in RANKS:
+        for j, (a, b) in enumerate(groups):
+            qu = SY if j % 2 == 0 else SC
+            prog[r].append((qu, 'W', 'g%d' % j))
+            prog[r].append((qu, 'ST', a, b))
+        prog[r].append((G, 'W', 'st'))
+    for c in prog:
+        if any(op[1] == 'S' for op in prog[c]):
+            prog[c].append((G, 'W', 'sent'))
+    tot = {}
+
+    def add(key, n):
+        tot[key] = tot.get(key, 0) + n
+    for c in prog:
+        for op in prog[c]:
+            if op[1] == 'S':
+                for p, dsts, mask, sem in op[2]:
+                    n = bin(mask).count('1')
+                    add((c, 'sent'), n)
+                    for d in dsts:
+                        add((d, sem), n)
+            elif op[1] == 'LD':
+                add((c, op[4]), 16)
+            elif op[1] in ('ST', 'XY'):
+                add((c, 'st'), 16)
+            elif op[1] == 'INC':
+                add((c, op[2]), 1)
+    return prog, tot
+
+
+PROG, TOTAL = build()
+SCRATCH = {'buf': ('dram', [NP, 128, NCOL], 'bfloat16')}
+SEMAPHORES = ['ld0', 'ld1', 'ld2', 'ld3', 'ld4', 'ld5', 'ld6', 'ld7', 'st', 'sent', 'pc', 'go',
+              'g0', 'g1', 'g2', 'g3', 'g4', 'g5', 'g6', 'g7', 'g8', 'g9']
+
 
 def rank_program(g, core, T, topo):
-    sems = {'ld0': T.sem.ld0, 'ld1': T.sem.ld1, 'ld2': T.sem.ld2, 'ld3': T.sem.ld3, 'st': T.sem.st, 'sent': T.sem.sent, 'pc': T.sem.pc, 'g0': T.sem.g0, 'g1': T.sem.g1, 'g2': T.sem.g2, 'g3': T.sem.g3, 'g4': T.sem.g4}
-    bufs = [T.bufa, T.bufb, T.bufc, T.bufd]
+    S = T.sem
+    sems = {'ld0': S.ld0, 'ld1': S.ld1, 'ld2': S.ld2, 'ld3': S.ld3, 'ld4': S.ld4, 'ld5': S.ld5,
+            'ld6': S.ld6, 'ld7': S.ld7, 'st': S.st, 'sent': S.sent, 'pc': S.pc, 'go': S.go,
+            'g0': S.g0, 'g1': S.g1, 'g2': S.g2, 'g3': S.g3, 'g4': S.g4, 'g5': S.g5, 'g6': S.g6,
+            'g7': S.g7, 'g8': S.g8, 'g9': S.g9}
+    qs = [g, g.sync, g.scalar]
+    buf = T.buf
     for op in PROG[core]:
-        if op[0] == 'W':
-            g.wait_ge(sems[op[1]], TOTAL[core, op[1]])
-        elif op[0] in ('LD', 'ST'):
-            b, lo, hi = (op[1], op[2], op[3])
-            r0 = ROW0[b] + lo * NCOLS[b] // 16
-            r1 = ROW0[b] + hi * NCOLS[b] // 16
-            if op[0] == 'LD':
-                g.dma_start(bufs[b][lo:hi], T.x[r0:r1, :]).then_inc(sems[op[4]], 16)
-            else:
-                g.dma_start(T.y[r0:r1, :], bufs[b][lo:hi]).then_inc(sems['st'], 16)
-        elif op[0] == 'XY':
-            g.dma_start(T.y[:, :], T.x[:, :]).then_inc(sems['st'], 16)
+        e = qs[op[0]]
+        kind = op[1]
+        if kind == 'W':
+            e.wait_ge(sems[op[2]], TOTAL[core, op[2]])
+        elif kind == 'INC':
+            e.sem_inc(sems[op[2]], 1)
+        elif kind == 'LD':
+            e.dma_start(buf[op[2]:op[3]], T.x[op[2] * RPP:op[3] * RPP, :]).then_inc(sems[op[4]], 16)
+        elif kind == 'ST':
+            e.dma_start(T.y[op[2] * RPP:op[3] * RPP, :], buf[op[2]:op[3]]).then_inc(sems['st'], 16)
+        elif kind == 'XY':
+            e.dma_start(T.y[:, :], T.x[:, :]).then_inc(sems['st'], 16)
         else:
             trs = []
-            for (b, s), dsts, mask, sem in op[1]:
+            for p, dsts, mask, sem in op[2]:
                 ids = [bass.DstId(rid=topo.addr(d)[0], pnc=topo.addr(d)[1]) for d in dsts]
-                trs.append(bass.RemoteDMATransfer(dst_ids=ids, dma_engine_mask=mask, remote_sem=sems[sem], srcs=[bufs[b][s]], dsts=[bufs[b][s] for d in dsts], alu_op=0))
+                trs.append(bass.RemoteDMATransfer(dst_ids=ids, dma_engine_mask=mask, remote_sem=sems[sem],
+                                                  srcs=[buf[p]], dsts=[buf[p] for d in dsts], alu_op=0))
             g.remote_dma_fused(trs, local_sem=sems['sent'])

@@ -8,12 +8,14 @@ ODD_R = [r for r in RANKS if r // 8 % 2 == 1]
 ODD = [1, 5, 7, 9, 11, 13, 15]
 HELP = [30, 26, 31, 27]
 SIDE = [24, 25, 24, 25]
-NP = 32
-NCOL = 64
-RPP = 128 // NP
-FAR = 4
-CHUNKS = [12, 8, 8, 4]
+D1 = [8 * c + 2 for c in ODD] + [8 * c + 3 for c in ODD]
+D0 = [8 * c + 6 for c in ODD] + [8 * c + 7 for c in ODD]
+HLIST = [c for w in range(3) for c in D1[4 * w:4 * w + 4] + D0[4 * w:4 * w + 4]]
+HLIST += [D1[12], D1[13], D1[7], D0[12], D0[13], D0[0], D0[1], D0[2]]
 G, SY, SC = 0, 1, 2
+WAVES = [(64, 8), (64, 8), (64, 8), (32, 8)]
+NF = 4
+NBUF = 6
 
 
 def eng(lo, n):
@@ -26,54 +28,62 @@ def rot(lst, core):
 
 def resend(core, piece, gname):
     ev, od = rot(EVEN_R, core), rot(ODD_R, core)
-    w = 8 // FAR
-    return [(piece, ev[s::FAR] + od[s::FAR], eng(s * w, w), gname) for s in range(FAR)]
+    return [(piece, ev[s::4] + od[s::4], eng(s * 2, 2), gname) for s in range(4)]
 
 
 def build():
     prog = {c: [] for c in range(128)}
     root = prog[ROOT]
-    lo = 0
-    bounds = []
-    for q, n in enumerate(CHUNKS):
-        root.append((SY if q % 2 == 0 else SC, 'LD', lo, lo + n, 'ld%d' % q))
-        bounds.append((lo, lo + n))
-        lo += n
-    groups = [(0, 4), (4, 12), (12, 20), (20, 28), (28, 32)]
-    first = [(i, [HELP[i], SIDE[i]], eng(8 + 2 * i, 2), 'pc') for i in range(4)]
+    row = 0
+    chunks = []
+    groups = []
+    for q, (n, cnt) in enumerate(WAVES):
+        tot = cnt + (NF if q == 0 else 0)
+        rpp = n // 16
+        chunks.append((q, 0, tot, row, row + tot * rpp))
+        if q == 0:
+            groups.append((q, 0, NF, row, row + NF * rpp))
+            groups.append((q, NF, tot, row + NF * rpp, row + tot * rpp))
+        else:
+            groups.append(chunks[-1])
+        row += tot * rpp
+    assert row == 128
+    for q, ch in enumerate(chunks):
+        root.append((SY if q % 2 == 0 else SC, 'LD', ch, 'ld%d' % q))
+    first = [((0, i), [HELP[i], SIDE[i]], eng(8 + 2 * i, 2), 'pc') for i in range(4)]
     for i in range(4):
         prog[HELP[i]].append((G, 'W', 'pc'))
-        prog[HELP[i]].append((G, 'S', [(i, EVEN_R[s::4], eng(s * 2, 2), 'g0') for s in range(4)]))
+        prog[HELP[i]].append((G, 'S', [((0, i), EVEN_R[s::4], eng(s * 2, 2), 'g0') for s in range(4)]))
     for s in range(2):
         prog[24 + s].append((G, 'W', 'pc'))
-        prog[24 + s].append((G, 'S', [(s + 2 * a, ODD_R[b::2], eng((a * 2 + b) * 2, 2), 'g0')
+        prog[24 + s].append((G, 'S', [((0, s + 2 * a), ODD_R[b::2], eng((a * 2 + b) * 2, 2), 'g0')
                                       for a in range(2) for b in range(2)]))
     k = 0
-    for q, (a, b) in enumerate(bounds):
-        base = a + 4 if q == 0 else a
-        cnt = b - base
+    own = {}
+    for q, (n, cnt) in enumerate(WAVES):
+        base = NF if q == 0 else 0
         wo = 8 // cnt
         trs = list(first) if q == 0 else []
         for i in range(cnt):
-            core = 8 * ODD[k % 7] + [2, 6, 3, 7][k // 7]
+            core = HLIST[k]
+            sem = 'pc2' if core in HLIST[:k] else 'pc'
             k += 1
-            trs.append((base + i, [core], eng(i * wo, wo), 'pc'))
-            prog[core].append((G, 'W', 'pc'))
+            trs.append(((q, base + i), [core], eng(i * wo, wo), sem))
+            prog[core].append((G, 'W', sem))
+            prog[core].append((G, 'S', resend(core, (q, base + i), 'g%d' % (q + 1))))
             if core in RANKS:
-                prog[core].append((SY, 'W', 'pc'))
-                prog[core].append((SC, 'W', 'pc'))
-            prog[core].append((G, 'S', resend(core, base + i, 'g%d' % (q + 1))))
+                assert core not in own
+                own[core] = q + 1
         root.append((G, 'W', 'ld%d' % q))
         root.append((G, 'S', trs))
-    root.append((G, 'INC', 'go'))
-    root.append((SY, 'W', 'go'))
-    root.append((SY, 'XY'))
-    root.append((G, 'W', 'st'))
+    root += [(G, 'INC', 'go'), (SY, 'W', 'go'), (SY, 'XY'), (G, 'W', 'st')]
     for r in RANKS:
-        for j, (a, b) in enumerate(groups):
+        for j, ch in enumerate(groups):
             qu = SY if j % 2 == 0 else SC
+            if own.get(r) == j:
+                prog[r].append((qu, 'W', 'pc'))
             prog[r].append((qu, 'W', 'g%d' % j))
-            prog[r].append((qu, 'ST', a, b))
+            prog[r].append((qu, 'ST', ch))
         prog[r].append((G, 'W', 'st'))
     for c in prog:
         if any(op[1] == 'S' for op in prog[c]):
@@ -91,28 +101,34 @@ def build():
                     for d in dsts:
                         add((d, sem), n)
             elif op[1] == 'LD':
-                add((c, op[4]), 16)
+                add((c, op[3]), 16)
             elif op[1] in ('ST', 'XY'):
                 add((c, 'st'), 16)
             elif op[1] == 'INC':
                 add((c, op[2]), 1)
-    return prog, tot
+    return prog, tot, chunks
 
 
-PROG, TOTAL = build()
-SCRATCH = {'buf': ('dram', [NP, 128, NCOL], 'bfloat16')}
-SEMAPHORES = ['ld0', 'ld1', 'ld2', 'ld3', 'ld4', 'ld5', 'ld6', 'ld7', 'st', 'sent', 'pc', 'go',
+PROG, TOTAL, CHUNKS = build()
+NCOL = {q: WAVES[q][0] for q in range(len(WAVES))}
+SCRATCH = {}
+for _q in range(NBUF):
+    if _q < len(WAVES):
+        SCRATCH['buf%d' % _q] = ('dram', [CHUNKS[_q][2], 128, WAVES[_q][0]], 'bfloat16')
+    else:
+        SCRATCH['buf%d' % _q] = ('dram', [1, 128, 16], 'bfloat16')
+SEMAPHORES = ['ld0', 'ld1', 'ld2', 'ld3', 'ld4', 'ld5', 'ld6', 'ld7', 'st', 'sent', 'pc', 'pc2', 'go',
               'g0', 'g1', 'g2', 'g3', 'g4', 'g5', 'g6', 'g7', 'g8', 'g9']
 
 
 def rank_program(g, core, T, topo):
     S = T.sem
     sems = {'ld0': S.ld0, 'ld1': S.ld1, 'ld2': S.ld2, 'ld3': S.ld3, 'ld4': S.ld4, 'ld5': S.ld5,
-            'ld6': S.ld6, 'ld7': S.ld7, 'st': S.st, 'sent': S.sent, 'pc': S.pc, 'go': S.go,
+            'ld6': S.ld6, 'ld7': S.ld7, 'st': S.st, 'sent': S.sent, 'pc': S.pc, 'pc2': S.pc2, 'go': S.go,
             'g0': S.g0, 'g1': S.g1, 'g2': S.g2, 'g3': S.g3, 'g4': S.g4, 'g5': S.g5, 'g6': S.g6,
             'g7': S.g7, 'g8': S.g8, 'g9': S.g9}
     qs = [g, g.sync, g.scalar]
-    buf = T.buf
+    bufs = [T.buf0, T.buf1, T.buf2, T.buf3, T.buf4, T.buf5]
     for op in PROG[core]:
         e = qs[op[0]]
         kind = op[1]
@@ -121,15 +137,17 @@ def rank_program(g, core, T, topo):
         elif kind == 'INC':
             e.sem_inc(sems[op[2]], 1)
         elif kind == 'LD':
-            e.dma_start(buf[op[2]:op[3]], T.x[op[2] * RPP:op[3] * RPP, :]).then_inc(sems[op[4]], 16)
+            b, lo, hi, r0, r1 = op[2]
+            e.dma_start(bufs[b][lo:hi], T.x[r0:r1, :]).then_inc(sems[op[3]], 16)
         elif kind == 'ST':
-            e.dma_start(T.y[op[2] * RPP:op[3] * RPP, :], buf[op[2]:op[3]]).then_inc(sems['st'], 16)
+            b, lo, hi, r0, r1 = op[2]
+            e.dma_start(T.y[r0:r1, :], bufs[b][lo:hi]).then_inc(sems['st'], 16)
         elif kind == 'XY':
             e.dma_start(T.y[:, :], T.x[:, :]).then_inc(sems['st'], 16)
         else:
             trs = []
-            for p, dsts, mask, sem in op[2]:
+            for (b, p), dsts, mask, sem in op[2]:
                 ids = [bass.DstId(rid=topo.addr(d)[0], pnc=topo.addr(d)[1]) for d in dsts]
                 trs.append(bass.RemoteDMATransfer(dst_ids=ids, dma_engine_mask=mask, remote_sem=sems[sem],
-                                                  srcs=[buf[p]], dsts=[buf[p] for d in dsts], alu_op=0))
+                                                  srcs=[bufs[b][p]], dsts=[bufs[b][p] for d in dsts], alu_op=0))
             g.remote_dma_fused(trs, local_sem=sems['sent'])

@@ -12,8 +12,9 @@ D1 = [8 * c + 2 for c in ODD] + [8 * c + 3 for c in ODD]
 D0 = [8 * c + 6 for c in ODD] + [8 * c + 7 for c in ODD]
 HLIST = [c for w in range(3) for c in D1[4 * w:4 * w + 4] + D0[4 * w:4 * w + 4]]
 HLIST += [D1[12], D1[13], D1[7], D0[12], D0[13], D0[0], D0[1], D0[2]]
+HLIST += D1[0:4] + D0[3:7]
 G, SY, SC = 0, 1, 2
-WAVES = [(64, 8), (64, 8), (64, 8), (32, 8)]
+WAVES = [(64, 8), (64, 8), (48, 8), (32, 8), (16, 8)]
 NF = 4
 NBUF = 6
 
@@ -72,16 +73,15 @@ def build():
             prog[core].append((G, 'W', sem))
             prog[core].append((G, 'S', resend(core, (q, base + i), 'g%d' % (q + 1))))
             if core in RANKS:
-                assert core not in own
-                own[core] = q + 1
+                own[core, q + 1] = sem
         root.append((G, 'W', 'ld%d' % q))
         root.append((G, 'S', trs))
     root += [(G, 'INC', 'go'), (SY, 'W', 'go'), (SY, 'XY'), (G, 'W', 'st')]
     for r in RANKS:
         for j, ch in enumerate(groups):
             qu = SY if j % 2 == 0 else SC
-            if own.get(r) == j:
-                prog[r].append((qu, 'W', 'pc'))
+            if (r, j) in own:
+                prog[r].append((qu, 'W', own[r, j]))
             prog[r].append((qu, 'W', 'g%d' % j))
             prog[r].append((qu, 'ST', ch))
         prog[r].append((G, 'W', 'st'))

import concourse.bass as bass
import comms_topo

ROOT = 29
RANKS = [8 * ch + 2 for ch in range(16) if ch != 3]
EVEN_R = [r for r in RANKS if r // 8 % 2 == 0]
ODD_R = [r for r in RANKS if r // 8 % 2 == 1]
ODD = [1, 5, 7, 9, 11, 13, 15]
HELP = [30, 26, 31, 27]
SIDE = [24, 25, 24, 25]
D1 = [8 * c + 2 for c in ODD] + [8 * c + 3 for c in ODD]
D0 = [8 * c + 6 for c in ODD] + [8 * c + 7 for c in ODD]
HLIST = [c for w in range(3) for c in D1[4 * w:4 * w + 4] + D0[4 * w:4 * w + 4]]
HLIST += [D1[12], D1[13], D1[7], D0[12], D0[13], D0[0], D0[1], D0[2]]
HLIST += D1[0:4] + D0[3:7]
G, SY, SC = 0, 1, 2
WAVES = [(64, 8), (64, 8), (48, 8), (32, 8), (16, 8)]
NF = 4
NBUF = 6


def eng(lo, n):
    return (1 << n) - 1 << lo


def rot(lst, core):
    return [r for r in lst if r > core] + [r for r in lst if r < core]


def resend(core, piece, gname):
    ev, od = rot(EVEN_R, core), rot(ODD_R, core)
    return [(piece, ev[s::4] + od[s::4], eng(s * 2, 2), gname) for s in range(4)]


def build():
    prog = {c: [] for c in range(128)}
    root = prog[ROOT]
    row = 0
    chunks = []
    groups = []
    for q, (n, cnt) in enumerate(WAVES):
        tot = cnt + (NF if q == 0 else 0)
        rpp = n // 16
        chunks.append((q, 0, tot, row, row + tot * rpp))
        if q == 0:
            groups.append((q, 0, NF, row, row + NF * rpp))
            groups.append((q, NF, tot, row + NF * rpp, row + tot * rpp))
        else:
            groups.append(chunks[-1])
        row += tot * rpp
    assert row == 128
    for q, ch in enumerate(chunks):
        root.append((SY if q % 2 == 0 else SC, 'LD', ch, 'ld%d' % q))
    first = [((0, i), [HELP[i], SIDE[i]], eng(8 + 2 * i, 2), 'pc') for i in range(4)]
    for i in range(4):
        prog[HELP[i]].append((G, 'W', 'pc'))
        prog[HELP[i]].append((G, 'S', [((0, i), EVEN_R[s::4], eng(s * 2, 2), 'g0') for s in range(4)]))
    for s in range(2):
        prog[24 + s].append((G, 'W', 'pc'))
        prog[24 + s].append((G, 'S', [((0, s + 2 * a), ODD_R[b::2], eng((a * 2 + b) * 2, 2), 'g0')
                                      for a in range(2) for b in range(2)]))
    k = 0
    own = {}
    for q, (n, cnt) in enumerate(WAVES):
        base = NF if q == 0 else 0
        wo = 8 // cnt
        trs = list(first) if q == 0 else []
        for i in range(cnt):
            core = HLIST[k]
            sem = 'pc2' if core in HLIST[:k] else 'pc'
            k += 1
            trs.append(((q, base + i), [core], eng(i * wo, wo), sem))
            prog[core].append((G, 'W', sem))
            prog[core].append((G, 'S', resend(core, (q, base + i), 'g%d' % (q + 1))))
            if core in RANKS:
                own[core, q + 1] = sem
        root.append((G, 'W', 'ld%d' % q))
        root.append((G, 'S', trs))
    root += [(G, 'INC', 'go'), (SY, 'W', 'go'), (SY, 'XY'), (G, 'W', 'st')]
    for r in RANKS:
        for j, ch in enumerate(groups):
            qu = SY if j % 2 == 0 else SC
            if (r, j) in own:
                prog[r].append((qu, 'W', own[r, j]))
            prog[r].append((qu, 'W', 'g%d' % j))
            prog[r].append((qu, 'ST', ch))
        prog[r].append((G, 'W', 'st'))
    for c in prog:
        if any(op[1] == 'S' for op in prog[c]):
            prog[c].append((G, 'W', 'sent'))
    tot = {}

    def add(key, n):
        tot[key] = tot.get(key, 0) + n
    for c in prog:
        for op in prog[c]:
            if op[1] == 'S':
                for p, dsts, mask, sem in op[2]:
                    n = bin(mask).count('1')
                    add((c, 'sent'), n)
                    for d in dsts:
                        add((d, sem), n)
            elif op[1] == 'LD':
                add((c, op[3]), 16)
            elif op[1] in ('ST', 'XY'):
                add((c, 'st'), 16)
            elif op[1] == 'INC':
                add((c, op[2]), 1)
    return prog, tot, chunks


PROG, TOTAL, CHUNKS = build()
NCOL = {q: WAVES[q][0] for q in range(len(WAVES))}
SCRATCH = {}
for _q in range(NBUF):
    if _q < len(WAVES):
        SCRATCH['buf%d' % _q] = ('dram', [CHUNKS[_q][2], 128, WAVES[_q][0]], 'bfloat16')
    else:
        SCRATCH['buf%d' % _q] = ('dram', [1, 128, 16], 'bfloat16')
SEMAPHORES = ['ld0', 'ld1', 'ld2', 'ld3', 'ld4', 'ld5', 'ld6', 'ld7', 'st', 'sent', 'pc', 'pc2', 'go',
              'g0', 'g1', 'g2', 'g3', 'g4', 'g5', 'g6', 'g7', 'g8', 'g9']


def rank_program(g, core, T, topo):
    S = T.sem
    sems = {'ld0': S.ld0, 'ld1': S.ld1, 'ld2': S.ld2, 'ld3': S.ld3, 'ld4': S.ld4, 'ld5': S.ld5,
            'ld6': S.ld6, 'ld7': S.ld7, 'st': S.st, 'sent': S.sent, 'pc': S.pc, 'pc2': S.pc2, 'go': S.go,
            'g0': S.g0, 'g1': S.g1, 'g2': S.g2, 'g3': S.g3, 'g4': S.g4, 'g5': S.g5, 'g6': S.g6,
            'g7': S.g7, 'g8': S.g8, 'g9': S.g9}
    qs = [g, g.sync, g.scalar]
    bufs = [T.buf0, T.buf1, T.buf2, T.buf3, T.buf4, T.buf5]
    for op in PROG[core]:
        e = qs[op[0]]
        kind = op[1]
        if kind == 'W':
            e.wait_ge(sems[op[2]], TOTAL[core, op[2]])
        elif kind == 'INC':
            e.sem_inc(sems[op[2]], 1)
        elif kind == 'LD':
            b, lo, hi, r0, r1 = op[2]
            e.dma_start(bufs[b][lo:hi], T.x[r0:r1, :]).then_inc(sems[op[3]], 16)
        elif kind == 'ST':
            b, lo, hi, r0, r1 = op[2]
            e.dma_start(T.y[r0:r1, :], bufs[b][lo:hi]).then_inc(sems['st'], 16)
        elif kind == 'XY':
            e.dma_start(T.y[:, :], T.x[:, :]).then_inc(sems['st'], 16)
        else:
            trs = []
            for (b, p), dsts, mask, sem in op[2]:
                ids = [bass.DstId(rid=topo.addr(d)[0], pnc=topo.addr(d)[1]) for d in dsts]
                trs.append(bass.RemoteDMATransfer(dst_ids=ids, dma_engine_mask=mask, remote_sem=sems[sem],
                                                  srcs=[bufs[b][p]], dsts=[bufs[b][p] for d in dsts], alu_op=0))
            g.remote_dma_fused(trs, local_sem=sems['sent'])
